import numpy as np
import ml_dtypes


def mxq(x, axis, fmt="e4m3"):
    dtype, down = {"e4m3": (ml_dtypes.float8_e4m3fn, 7), "e5m2": (ml_dtypes.float8_e5m2, 14)}[fmt]
    v = np.moveaxis(np.asarray(x, np.float32).astype(ml_dtypes.bfloat16).astype(np.float64), axis, -1)
    blocks = v.reshape(v.shape[:-1] + (-1, 32))
    amax = np.abs(blocks).max(-1, keepdims=True)
    byte = np.maximum(np.where(amax > 0, np.frexp(amax)[1] - 1 + 127, 0) - down, 1)
    scale = np.exp2(byte - 127.0)
    codes = (blocks / scale).astype(np.float32).astype(dtype).astype(np.float64)
    return np.moveaxis((codes * scale).reshape(v.shape), -1, axis)


WIDE = False


def mx_kscale(k):
    if not WIDE:
        return np.ones(k)
    levels = np.array([30, -30])
    if k % 512:
        return np.exp2(np.random.permutation(np.resize(levels, k // 32))).repeat(32)
    a = np.empty((k // 512, 16))
    for p in range(k // 512):
        a[p, :8] = np.random.permutation(np.resize(levels, 8))
        for g in range(8):
            far = levels[np.abs(levels - a[p, g]) >= 10]
            a[p, g + 8] = far[np.random.randint(len(far))]
    return np.exp2(a.ravel()).repeat(32)


def f64(x):
    return np.asarray(x).astype(np.float64)


def striped(idx):
    return np.tile(np.asarray(idx).reshape(-1, 16).T, (8, 1)).astype(np.uint16)


def unstriped(offs):
    return offs[:16].T.reshape(-1).astype(np.int64)


E2M1 = np.array([0.0, 0.5, 1.0, 1.5, 2.0, 3.0, 4.0, 6.0, -0.0, -0.5, -1.0, -1.5, -2.0, -3.0, -4.0, -6.0])


def pack_weight(w, fmt):
    k, n = w.shape
    w = f64(np.asarray(w, np.float32).astype(ml_dtypes.bfloat16)).reshape(k // 32, 32, n)
    amax = np.abs(w).max(1)
    if fmt in ("e4m3", "e5m2"):
        byte = np.frexp(amax)[1] - 1 + 127 - (7 if fmt == "e4m3" else 14)
    else:
        mant, ex = np.frexp(amax / 6.0)
        byte = np.where(mant > 0.5, ex, ex - 1) + 127
    byte = np.clip(np.where(amax > 0, byte, 1), 1, 254)
    scaled = (w * np.exp2(127.0 - byte)[:, None, :]).reshape(k, n).astype(np.float32)
    by_word = np.ascontiguousarray(scaled.reshape(k // 512, 128, 4, n).transpose(0, 1, 3, 2))
    if fmt in ("e4m3", "e5m2"):
        words = by_word.astype(ml_dtypes.float8_e4m3fn if fmt == "e4m3" else ml_dtypes.float8_e5m2).view(np.uint8)
    else:
        c = by_word.astype(ml_dtypes.float4_e2m1fn).view(np.uint8) & 0xF
        words = (c[..., 0::2] | (c[..., 1::2] << 4)).reshape(k // 512, 128, 2 * n)
    return np.ascontiguousarray(words), np.ascontiguousarray(byte.astype(np.uint8).reshape(k // 512, 16, n))


def unpack_weight(words, scales, fmt):
    g, _, n = scales.shape
    words = np.ascontiguousarray(words).reshape(g, 128, n, -1)
    if fmt in ("e4m3", "e5m2"):
        vals = words.view(ml_dtypes.float8_e4m3fn if fmt == "e4m3" else ml_dtypes.float8_e5m2).astype(np.float64)
    else:
        nib = np.empty((g, 128, n, 4), np.uint8)
        nib[..., 0::2] = words & 0xF
        nib[..., 1::2] = words >> 4
        vals = E2M1[nib]
    vals = vals * np.repeat(np.exp2(scales.astype(np.float64) - 127.0), 8, axis=1)[..., None]
    return vals.transpose(0, 1, 3, 2).reshape(g * 512, n)


K, T, J, I, V = 1024, 1024, 256, 256, 1024


def setup_inputs():
    n = np.random.standard_normal
    idx = np.random.permutation(T)[:J]
    idx2 = np.random.permutation(V)[:I]
    fk = mx_kscale(K)
    xtp = pack_weight(n((K, T)) * 0.04 * fk[:, None], "e5m2")
    return {
        "xt_words": xtp[0],
        "xt_scales": xtp[1],
        "kf": (n((K, V))).astype(np.float32),
        "ko": (n((K, I)) * 0.6).astype(np.float32),
        "fi": (np.random.uniform(0.5, 2.0, (K, 1)) / fk[:, None]).astype(np.float32),
        "bi": (np.random.uniform(-0.7, 0.7, (1, I))).astype(np.float32),
        "tg": (np.random.uniform(-0.5, 1.5, (J, 1))).astype(np.float32),
        "offs": striped(idx),
        "offs2": striped(idx2),
    }


def reference(xt_words, xt_scales, kf, ko, fi, bi, tg, offs, offs2):
    idx = unstriped(offs)
    idx2 = unstriped(offs2)
    xtu = unpack_weight(xt_words, xt_scales, "e5m2")
    vk = (f64(kf)[:, idx2] + f64(ko)) * f64(fi)
    xtidxg = xtu[:, idx]
    vkq = mxq(vk, 0, "e5m2")
    a0 = xtidxg.T @ vkq
    a = a0 + f64(bi)
    y = np.square(np.maximum(a - f64(tg), 0.0))
    return y

@@ -1,0 +1,156 @@
+from contextlib import ExitStack
+
+import concourse.mybir as mybir
+from concourse.masks import make_identity
+
+K, T, J, I, V = 1024, 1024, 256, 256, 1024
+FLOPS = 2 * K * J * I
+
+F32 = mybir.dt.float32
+BF16 = mybir.dt.bfloat16
+I32 = mybir.dt.int32
+U32 = mybir.dt.uint32
+U16 = mybir.dt.uint16
+U8 = mybir.dt.uint8
+E5M2X4 = mybir.dt.float8_e5m2_x4
+ALU = mybir.AluOpType
+COPY = mybir.ActivationFunctionType.Copy
+
+P = 128
+PACK = 4
+PASSES = K // (P * PACK)
+HALVES = J // P
+QUADS = 4
+SLOTS = 5
+
+
+def tile_list_scores_picked_mixed_hinge_kernel(tc, xt_words, xt_scales, kf, ko, fi, bi, tg, offs, offs2, out):
+    nc = tc.nc
+    with ExitStack() as ctx:
+        keep = ctx.enter_context(tc.tile_pool(name="keep", bufs=1))
+        ring = ctx.enter_context(tc.tile_pool(name="ring", bufs=4))
+        stream = ctx.enter_context(tc.tile_pool(name="stream", bufs=1))
+        psum = ctx.enter_context(tc.psum_pool(name="psum", bufs=1))
+
+        tok_list = keep.tile([P, J // 16], U16, name="tok_list")
+        key_list = keep.tile([P, I // 16], U16, name="key_list")
+        store = [[stream.tile([P, V], F32, name="store_%d_%d" % (z, r), tag="slot_%d" % ((z * PACK + r) % SLOTS), align_bytes=64) for r in range(PACK)] for z in range(PASSES)]
+        own = [keep.tile([P, PACK, I], F32, name="own_%d" % z) for z in range(PASSES)]
+        words = [stream.tile([P, T], U32, name="words_%d" % z, tag="slot_%d" % ((PASSES * PACK + z) % SLOTS), align_bytes=64) for z in range(PASSES)]
+        scales = keep.tile([P, PASSES * T], U8, name="scales")
+        factor = keep.tile([P, PASSES, 8], F32, name="factor")
+        bias_pairs = keep.tile([P, 2], F32, name="bias_pairs")
+        target_pairs = keep.tile([P, 2], F32, name="target_pairs")
+        ident = keep.tile([P, P], F32, name="ident")
+
+        kf_planes = kf.rearrange("(z p r) v -> z r p v", z=PASSES, r=PACK)
+        ko_passes = ko.rearrange("(z p r) i -> z p r i", z=PASSES, r=PACK)
+
+        def load_store(n):
+            nc.sync.dma_start(store[n // PACK][n % PACK][:], kf_planes[n // PACK, n % PACK])
+
+        def load_scales(q):
+            nc.sync.dma_start(
+                scales[32 * q : 32 * q + 4, :].bitcast(I32).rearrange("r (z c) -> r z c", z=PASSES),
+                xt_scales[:, 4 * q : 4 * q + 4, :].bitcast(I32).rearrange("z r c -> r z c"),
+            )
+
+        def load_words(z):
+            nc.sync.dma_start(words[z][:].bitcast(I32), xt_words[z].rearrange("p c r -> p (c r)").bitcast(I32))
+
+        nc.vector.memset(scales[:].bitcast(I32), 0)
+        make_identity(nc, ident[:])
+
+        nc.scalar.dma_start(bias_pairs[:], bi.rearrange("o (p e) -> (o p) e", e=2))
+        nc.scalar.dma_start(target_pairs[:], tg.rearrange("(p e) o -> p (e o)", e=2))
+        nc.scalar.dma_start(factor[:, :, 0:PACK], fi.rearrange("(z p r) o -> p z (r o)", z=PASSES, r=PACK))
+        nc.sync.dma_start(own[0][:], ko_passes[0])
+        nc.sync.dma_start(key_list[:], offs2)
+        load_store(0)
+        nc.sync.dma_start(tok_list[:], offs)
+        load_store(1)
+        load_store(2)
+        load_scales(0)
+        load_store(3)
+        load_scales(1)
+        load_scales(2)
+        nc.sync.dma_start(own[1][:], ko_passes[1])
+        load_scales(3)
+        for n in range(PACK, PASSES * PACK):
+            load_store(n)
+        for z in range(PASSES):
+            load_words(z)
+
+        def spread_row(pairs, name):
+            bank = psum.tile([P, 2, P], F32, name=name + "_bank")
+            for e in range(2):
+                nc.tensor.transpose(bank[:, e, :], pairs[:, e : e + 1].to_broadcast([P, P]), ident[:])
+            row = keep.tile([P, 2 * P], F32, name=name + "_row")
+            nc.scalar.activation(row[:].rearrange("p (n e) -> p n e", e=2), bank[:].rearrange("p e n -> p n e"), COPY)
+            return row
+
+        woven = [keep.tile([P, I, PACK], BF16, name="woven_%d" % z, align_bytes=64) for z in range(PASSES)]
+        key_codes = [stream.tile([P, I], U32, name="key_codes_%d" % z, tag="slot_%d" % (3 * z), align_bytes=64) for z in range(PASSES)]
+        key_scales = [keep.tile([P, I], U8, name="key_scales_%d" % z, align_bytes=64) for z in range(PASSES)]
+        tok_scales = [keep.tile([P, J], U8, name="tok_scales_%d" % z, align_bytes=64) for z in range(PASSES)]
+        first = keep.tile([P, J], U32, name="tok_words_0", align_bytes=64)
+
+        def make_plane(z, r):
+            summed = ring.tile([P, I], F32, name="summed")
+            nc.vector.tensor_tensor(summed[:], store[z][r][:].indirect(key_list[:]), own[z][:, r, :], ALU.add)
+            nc.scalar.activation(woven[z][:, :, r], summed[:], COPY, scale=factor[:, z, r : r + 1])
+
+        def quantize(z):
+            nc.vector.quantize_mx(key_codes[z][:].bitcast(E5M2X4), key_scales[z][:], woven[z][:].rearrange("p i r -> p (i r)"))
+
+        bias_row = spread_row(bias_pairs, "bias")
+        target_row = spread_row(target_pairs, "target")
+        target_bank = psum.tile([P, HALVES, P], F32, name="target_col_bank")
+        for h in range(HALVES):
+            nc.tensor.transpose(target_bank[:, h, :], target_row[:, h * P : (h + 1) * P], ident[:])
+        target_col = keep.tile([P, HALVES], F32, name="target_col")
+        nc.scalar.activation(target_col[:], target_bank[:, :, 0], COPY)
+
+        for r in range(PACK):
+            make_plane(0, r)
+        for z in range(PASSES):
+            nc.vector.tensor_copy(tok_scales[z][:], scales[:, z * T : (z + 1) * T].indirect(tok_list[:]))
+        make_plane(1, 0)
+        make_plane(1, 1)
+        quantize(0)
+        for r in range(2, PACK):
+            make_plane(1, r)
+        nc.vector.tensor_copy(first[:], words[0][:].indirect(tok_list[:]))
+        quantize(1)
+        acc = [psum.tile([P, I], F32, name="acc_%d" % h) for h in range(HALVES)]
+        for h in range(HALVES):
+            nc.tensor.matmul_mx(
+                acc[h][:],
+                lhsT=first[:, h * P : (h + 1) * P].bitcast(E5M2X4),
+                lhsT_scale=tok_scales[0][:, h * P : (h + 1) * P],
+                rhs=key_codes[0][:].bitcast(E5M2X4),
+                rhs_scale=key_scales[0][:],
+                start=True,
+                stop=False,
+            )
+        for h in range(HALVES):
+            last = keep.tile([P, P], U32, name="tok_words_1_%d" % h, align_bytes=64)
+            nc.vector.tensor_copy(last[:], words[1][:].indirect(tok_list[:, h * (P // 16) : (h + 1) * (P // 16)]))
+            nc.tensor.matmul_mx(
+                acc[h][:],
+                lhsT=last[:].bitcast(E5M2X4),
+                lhsT_scale=tok_scales[1][:, h * P : (h + 1) * P],
+                rhs=key_codes[1][:].bitcast(E5M2X4),
+                rhs_scale=key_scales[1][:],
+                start=False,
+                stop=True,
+            )
+        excess = []
+        for h in range(HALVES):
+            over = keep.tile([P, I], F32, name="excess_%d" % h)
+            nc.vector.scalar_tensor_tensor(over[:], acc[h][:], target_col[:, h : h + 1], bias_row[:], ALU.subtract, ALU.add)
+            excess.append(over)
+        for h in range(HALVES):
+            result = keep.tile([P, I], F32, name="result_%d" % h)
+            nc.vector.scalar_tensor_tensor(result[:], excess[h][:], 0.0, excess[h][:], ALU.max, ALU.mult)
+            nc.sync.dma_start(out[h * P : (h + 1) * P, :], result[:])

@@ -21,7 +21,7 @@ PACK = 4
 PASSES = K // (P * PACK)
 HALVES = J // P
 QUADS = 4
-SLOTS = 5
+FACTOR_ROW, BIAS_ROW, TARGET_ROW = 20, 28, 29
 
 
 def tile_list_scores_picked_mixed_hinge_kernel(tc, xt_words, xt_scales, kf, ko, fi, bi, tg, offs, offs2, out):
@@ -29,25 +29,23 @@ def tile_list_scores_picked_mixed_hinge_kernel(tc, xt_words, xt_scales, kf, ko, 
     with ExitStack() as ctx:
         keep = ctx.enter_context(tc.tile_pool(name="keep", bufs=1))
         ring = ctx.enter_context(tc.tile_pool(name="ring", bufs=4))
-        stream = ctx.enter_context(tc.tile_pool(name="stream", bufs=1))
         psum = ctx.enter_context(tc.psum_pool(name="psum", bufs=1))
 
         tok_list = keep.tile([P, J // 16], U16, name="tok_list")
         key_list = keep.tile([P, I // 16], U16, name="key_list")
-        store = [[stream.tile([P, V], F32, name="store_%d_%d" % (z, r), tag="slot_%d" % ((z * PACK + r) % SLOTS), align_bytes=64) for r in range(PACK)] for z in range(PASSES)]
+        store = [keep.tile([P, V], F32, name="store_%d" % n, tag="store_%d" % n, align_bytes=64) for n in range(PASSES * PACK)]
         own = [keep.tile([P, PACK, I], F32, name="own_%d" % z) for z in range(PASSES)]
-        words = [stream.tile([P, T], U32, name="words_%d" % z, tag="slot_%d" % ((PASSES * PACK + z) % SLOTS), align_bytes=64) for z in range(PASSES)]
+        words = [keep.tile([P, T], U32, name="words_%d" % z, tag="words_%d" % z, align_bytes=64) for z in range(PASSES)]
         scales = keep.tile([P, PASSES * T], U8, name="scales")
-        factor = keep.tile([P, PASSES, 8], F32, name="factor")
-        bias_pairs = keep.tile([P, 2], F32, name="bias_pairs")
-        target_pairs = keep.tile([P, 2], F32, name="target_pairs")
+        rows = keep.tile([P, P * PACK], F32, name="rows")
         ident = keep.tile([P, P], F32, name="ident")
+        tok_scales = [keep.tile([P, J], U8, name="tok_scales_%d" % z, align_bytes=64) for z in range(PASSES)]
 
         kf_planes = kf.rearrange("(z p r) v -> z r p v", z=PASSES, r=PACK)
         ko_passes = ko.rearrange("(z p r) i -> z p r i", z=PASSES, r=PACK)
 
         def load_store(n):
-            nc.sync.dma_start(store[n // PACK][n % PACK][:], kf_planes[n // PACK, n % PACK])
+            nc.sync.dma_start(store[n][:], kf_planes[n // PACK, n % PACK])
 
         def load_scales(q):
             nc.sync.dma_start(
@@ -55,19 +53,17 @@ def tile_list_scores_picked_mixed_hinge_kernel(tc, xt_words, xt_scales, kf, ko, 
                 xt_scales[:, 4 * q : 4 * q + 4, :].bitcast(I32).rearrange("z r c -> r z c"),
             )
 
-        def load_words(z):
-            nc.sync.dma_start(words[z][:].bitcast(I32), xt_words[z].rearrange("p c r -> p (c r)").bitcast(I32))
-
+        nc.vector.memset(rows[:], 0.0)
         nc.vector.memset(scales[:].bitcast(I32), 0)
         make_identity(nc, ident[:])
 
-        nc.scalar.dma_start(bias_pairs[:], bi.rearrange("o (p e) -> (o p) e", e=2))
-        nc.scalar.dma_start(target_pairs[:], tg.rearrange("(p e) o -> p (e o)", e=2))
-        nc.scalar.dma_start(factor[:, :, 0:PACK], fi.rearrange("(z p r) o -> p z (r o)", z=PASSES, r=PACK))
         nc.sync.dma_start(own[0][:], ko_passes[0])
         nc.sync.dma_start(key_list[:], offs2)
         load_store(0)
         nc.sync.dma_start(tok_list[:], offs)
+        nc.sync.dma_start(rows[FACTOR_ROW : FACTOR_ROW + PASSES, :], fi.rearrange("(z k) o -> z (k o)", z=PASSES))
+        nc.sync.dma_start(rows[BIAS_ROW : BIAS_ROW + 1, 0:I], bi)
+        nc.sync.dma_start(rows[TARGET_ROW : TARGET_ROW + 1, 0:J], tg.rearrange("j o -> o j"))
         load_store(1)
         load_store(2)
         load_scales(0)
@@ -79,47 +75,54 @@ def tile_list_scores_picked_mixed_hinge_kernel(tc, xt_words, xt_scales, kf, ko, 
         for n in range(PACK, PASSES * PACK):
             load_store(n)
         for z in range(PASSES):
-            load_words(z)
+            nc.sync.dma_start(words[z][:].bitcast(I32), xt_words[z].rearrange("p c r -> p (c r)").bitcast(I32))
 
-        def spread_row(pairs, name):
-            bank = psum.tile([P, 2, P], F32, name=name + "_bank")
-            for e in range(2):
-                nc.tensor.transpose(bank[:, e, :], pairs[:, e : e + 1].to_broadcast([P, P]), ident[:])
-            row = keep.tile([P, 2 * P], F32, name=name + "_row")
-            nc.scalar.activation(row[:].rearrange("p (n e) -> p n e", e=2), bank[:].rearrange("p e n -> p n e"), COPY)
-            return row
+        factor_bank = psum.tile([P, PACK, P], F32, name="factor_bank")
+        for r in range(PACK):
+            nc.tensor.transpose(factor_bank[:, r, :], rows[:, r : P * PACK : PACK], ident[:])
+        factor = keep.tile([P, PACK, PASSES], F32, name="factor")
+        nc.scalar.activation(factor[:], factor_bank[:, :, FACTOR_ROW : FACTOR_ROW + PASSES], COPY)
+        cols_bank = psum.tile([P, HALVES, P], F32, name="cols_bank")
+        for h in range(HALVES):
+            nc.tensor.transpose(cols_bank[:, h, :], rows[:, h * P : (h + 1) * P], ident[:])
+        cols = keep.tile([P, HALVES, 2], F32, name="cols")
+        nc.scalar.activation(cols[:], cols_bank[:, :, BIAS_ROW : BIAS_ROW + 2], COPY)
+        bias_bank = psum.tile([P, I], F32, name="bias_bank")
+        for h in range(HALVES):
+            nc.tensor.transpose(bias_bank[:, h * P : (h + 1) * P], cols[:, h, 0:1].to_broadcast([P, P]), ident[:])
+        bias_row = keep.tile([P, I], F32, name="bias_row")
+        nc.scalar.activation(bias_row[:], bias_bank[:], COPY)
 
         woven = [keep.tile([P, I, PACK], BF16, name="woven_%d" % z, align_bytes=64) for z in range(PASSES)]
-        key_codes = [stream.tile([P, I], U32, name="key_codes_%d" % z, tag="slot_%d" % (3 * z), align_bytes=64) for z in range(PASSES)]
+        key_codes = [
+            keep.tile([P, I], U32, name="key_codes_0", tag="store_5", align_bytes=64),
+            keep.tile([P, I], U32, name="key_codes_1", tag="words_0", align_bytes=64),
+        ]
         key_scales = [keep.tile([P, I], U8, name="key_scales_%d" % z, align_bytes=64) for z in range(PASSES)]
-        tok_scales = [keep.tile([P, J], U8, name="tok_scales_%d" % z, align_bytes=64) for z in range(PASSES)]
         first = keep.tile([P, J], U32, name="tok_words_0", align_bytes=64)
 
-        def make_plane(z, r):
-            summed = ring.tile([P, I], F32, name="summed")
-            nc.vector.tensor_tensor(summed[:], store[z][r][:].indirect(key_list[:]), own[z][:, r, :], ALU.add)
-            nc.scalar.activation(woven[z][:, :, r], summed[:], COPY, scale=factor[:, z, r : r + 1])
+        def make_plane(n, pieces):
+            z, r = divmod(n, PACK)
+            width = I // pieces
+            for c in range(pieces):
+                part = slice(c * width, (c + 1) * width)
+                listed = key_list[:, c * width // 16 : (c + 1) * width // 16]
+                summed = ring.tile([P, width], F32, name="summed")
+                nc.vector.tensor_tensor(summed[:], store[n][:].indirect(listed), own[z][:, r, part], ALU.add)
+                nc.scalar.activation(woven[z][:, part, r], summed[:], COPY, scale=factor[:, r, z : z + 1])
 
         def quantize(z):
             nc.vector.quantize_mx(key_codes[z][:].bitcast(E5M2X4), key_scales[z][:], woven[z][:].rearrange("p i r -> p (i r)"))
 
-        bias_row = spread_row(bias_pairs, "bias")
-        target_row = spread_row(target_pairs, "target")
-        target_bank = psum.tile([P, HALVES, P], F32, name="target_col_bank")
-        for h in range(HALVES):
-            nc.tensor.transpose(target_bank[:, h, :], target_row[:, h * P : (h + 1) * P], ident[:])
-        target_col = keep.tile([P, HALVES], F32, name="target_col")
-        nc.scalar.activation(target_col[:], target_bank[:, :, 0], COPY)
-
-        for r in range(PACK):
-            make_plane(0, r)
+        for n in range(PACK):
+            make_plane(n, 1)
         for z in range(PASSES):
             nc.vector.tensor_copy(tok_scales[z][:], scales[:, z * T : (z + 1) * T].indirect(tok_list[:]))
-        make_plane(1, 0)
-        make_plane(1, 1)
+        make_plane(PACK, 1)
+        make_plane(PACK + 1, 1)
         quantize(0)
-        for r in range(2, PACK):
-            make_plane(1, r)
+        make_plane(PACK + 2, 1)
+        make_plane(PACK + 3, 2)
         nc.vector.tensor_copy(first[:], words[0][:].indirect(tok_list[:]))
         quantize(1)
         acc = [psum.tile([P, I], F32, name="acc_%d" % h) for h in range(HALVES)]
@@ -148,7 +151,7 @@ def tile_list_scores_picked_mixed_hinge_kernel(tc, xt_words, xt_scales, kf, ko, 
         excess = []
         for h in range(HALVES):
             over = keep.tile([P, I], F32, name="excess_%d" % h)
-            nc.vector.scalar_tensor_tensor(over[:], acc[h][:], target_col[:, h : h + 1], bias_row[:], ALU.subtract, ALU.add)
+            nc.vector.scalar_tensor_tensor(over[:], acc[h][:], cols[:, h, 1:2], bias_row[:], ALU.subtract, ALU.add)
             excess.append(over)
         for h in range(HALVES):
             result = keep.tile([P, I], F32, name="result_%d" % h)

from contextlib import ExitStack

import concourse.mybir as mybir
from concourse.masks import make_identity

K, T, J, I, V = 1024, 1024, 256, 256, 1024
FLOPS = 2 * K * J * I

F32 = mybir.dt.float32
BF16 = mybir.dt.bfloat16
I32 = mybir.dt.int32
U32 = mybir.dt.uint32
U16 = mybir.dt.uint16
U8 = mybir.dt.uint8
E5M2X4 = mybir.dt.float8_e5m2_x4
ALU = mybir.AluOpType
COPY = mybir.ActivationFunctionType.Copy

P = 128
PACK = 4
PASSES = K // (P * PACK)
HALVES = J // P
QUADS = 4
FACTOR_ROW, BIAS_ROW, TARGET_ROW = 20, 28, 29


def tile_list_scores_picked_mixed_hinge_kernel(tc, xt_words, xt_scales, kf, ko, fi, bi, tg, offs, offs2, out):
    nc = tc.nc
    with ExitStack() as ctx:
        keep = ctx.enter_context(tc.tile_pool(name="keep", bufs=1))
        ring = ctx.enter_context(tc.tile_pool(name="ring", bufs=4))
        psum = ctx.enter_context(tc.psum_pool(name="psum", bufs=1))

        tok_list = keep.tile([P, J // 16], U16, name="tok_list")
        key_list = keep.tile([P, I // 16], U16, name="key_list")
        store = [keep.tile([P, V], F32, name="store_%d" % n, tag="store_%d" % n, align_bytes=64) for n in range(PASSES * PACK)]
        own = [keep.tile([P, PACK, I], F32, name="own_%d" % z) for z in range(PASSES)]
        words = [keep.tile([P, T], U32, name="words_%d" % z, tag="words_%d" % z, align_bytes=64) for z in range(PASSES)]
        scales = keep.tile([P, PASSES * T], U8, name="scales")
        rows = keep.tile([P, P * PACK], F32, name="rows")
        ident = keep.tile([P, P], F32, name="ident")
        tok_scales = [keep.tile([P, J], U8, name="tok_scales_%d" % z, align_bytes=64) for z in range(PASSES)]

        kf_planes = kf.rearrange("(z p r) v -> z r p v", z=PASSES, r=PACK)
        ko_passes = ko.rearrange("(z p r) i -> z p r i", z=PASSES, r=PACK)

        def load_store(n):
            nc.sync.dma_start(store[n][:], kf_planes[n // PACK, n % PACK])

        def load_scales(q):
            nc.sync.dma_start(
                scales[32 * q : 32 * q + 4, :].bitcast(I32).rearrange("r (z c) -> r z c", z=PASSES),
                xt_scales[:, 4 * q : 4 * q + 4, :].bitcast(I32).rearrange("z r c -> r z c"),
            )

        nc.vector.memset(rows[:], 0.0)
        nc.vector.memset(scales[:].bitcast(I32), 0)
        make_identity(nc, ident[:])

        nc.sync.dma_start(own[0][:], ko_passes[0])
        nc.sync.dma_start(key_list[:], offs2)
        load_store(0)
        nc.sync.dma_start(tok_list[:], offs)
        nc.sync.dma_start(rows[FACTOR_ROW : FACTOR_ROW + PASSES, :], fi.rearrange("(z k) o -> z (k o)", z=PASSES))
        nc.sync.dma_start(rows[BIAS_ROW : BIAS_ROW + 1, 0:I], bi)
        nc.sync.dma_start(rows[TARGET_ROW : TARGET_ROW + 1, 0:J], tg.rearrange("j o -> o j"))
        load_store(1)
        load_store(2)
        load_scales(0)
        load_store(3)
        load_scales(1)
        load_scales(2)
        nc.sync.dma_start(own[1][:], ko_passes[1])
        load_scales(3)
        for n in range(PACK, PASSES * PACK):
            load_store(n)
        for z in range(PASSES):
            nc.sync.dma_start(words[z][:].bitcast(I32), xt_words[z].rearrange("p c r -> p (c r)").bitcast(I32))

        factor_bank = psum.tile([P, PACK, P], F32, name="factor_bank")
        for r in range(PACK):
            nc.tensor.transpose(factor_bank[:, r, :], rows[:, r : P * PACK : PACK], ident[:])
        factor = keep.tile([P, PACK, PASSES], F32, name="factor")
        nc.scalar.activation(factor[:], factor_bank[:, :, FACTOR_ROW : FACTOR_ROW + PASSES], COPY)
        cols_bank = psum.tile([P, HALVES, P], F32, name="cols_bank")
        for h in range(HALVES):
            nc.tensor.transpose(cols_bank[:, h, :], rows[:, h * P : (h + 1) * P], ident[:])
        cols = keep.tile([P, HALVES, 2], F32, name="cols")
        nc.scalar.activation(cols[:], cols_bank[:, :, BIAS_ROW : BIAS_ROW + 2], COPY)
        bias_bank = psum.tile([P, I], F32, name="bias_bank")
        for h in range(HALVES):
            nc.tensor.transpose(bias_bank[:, h * P : (h + 1) * P], cols[:, h, 0:1].to_broadcast([P, P]), ident[:])
        bias_row = keep.tile([P, I], F32, name="bias_row")
        nc.scalar.activation(bias_row[:], bias_bank[:], COPY)

        woven = [keep.tile([P, I, PACK], BF16, name="woven_%d" % z, align_bytes=64) for z in range(PASSES)]
        key_codes = [
            keep.tile([P, I], U32, name="key_codes_0", tag="store_5", align_bytes=64),
            keep.tile([P, I], U32, name="key_codes_1", tag="words_0", align_bytes=64),
        ]
        key_scales = [keep.tile([P, I], U8, name="key_scales_%d" % z, align_bytes=64) for z in range(PASSES)]
        first = keep.tile([P, J], U32, name="tok_words_0", align_bytes=64)

        def make_plane(n, pieces):
            z, r = divmod(n, PACK)
            width = I // pieces
            for c in range(pieces):
                part = slice(c * width, (c + 1) * width)
                listed = key_list[:, c * width // 16 : (c + 1) * width // 16]
                summed = ring.tile([P, width], F32, name="summed")
                nc.vector.tensor_tensor(summed[:], store[n][:].indirect(listed), own[z][:, r, part], ALU.add)
                nc.scalar.activation(woven[z][:, part, r], summed[:], COPY, scale=factor[:, r, z : z + 1])

        def quantize(z):
            nc.vector.quantize_mx(key_codes[z][:].bitcast(E5M2X4), key_scales[z][:], woven[z][:].rearrange("p i r -> p (i r)"))

        for n in range(PACK):
            make_plane(n, 1)
        for z in range(PASSES):
            nc.vector.tensor_copy(tok_scales[z][:], scales[:, z * T : (z + 1) * T].indirect(tok_list[:]))
        make_plane(PACK, 1)
        make_plane(PACK + 1, 1)
        quantize(0)
        make_plane(PACK + 2, 1)
        make_plane(PACK + 3, 2)
        nc.vector.tensor_copy(first[:], words[0][:].indirect(tok_list[:]))
        quantize(1)
        acc = [psum.tile([P, I], F32, name="acc_%d" % h) for h in range(HALVES)]
        for h in range(HALVES):
            nc.tensor.matmul_mx(
                acc[h][:],
                lhsT=first[:, h * P : (h + 1) * P].bitcast(E5M2X4),
                lhsT_scale=tok_scales[0][:, h * P : (h + 1) * P],
                rhs=key_codes[0][:].bitcast(E5M2X4),
                rhs_scale=key_scales[0][:],
                start=True,
                stop=False,
            )
        for h in range(HALVES):
            last = keep.tile([P, P], U32, name="tok_words_1_%d" % h, align_bytes=64)
            nc.vector.tensor_copy(last[:], words[1][:].indirect(tok_list[:, h * (P // 16) : (h + 1) * (P // 16)]))
            nc.tensor.matmul_mx(
                acc[h][:],
                lhsT=last[:].bitcast(E5M2X4),
                lhsT_scale=tok_scales[1][:, h * P : (h + 1) * P],
                rhs=key_codes[1][:].bitcast(E5M2X4),
                rhs_scale=key_scales[1][:],
                start=False,
                stop=True,
            )
        excess = []
        for h in range(HALVES):
            over = keep.tile([P, I], F32, name="excess_%d" % h)
            nc.vector.scalar_tensor_tensor(over[:], acc[h][:], cols[:, h, 1:2], bias_row[:], ALU.subtract, ALU.add)
            excess.append(over)
        for h in range(HALVES):
            result = keep.tile([P, I], F32, name="result_%d" % h)
            nc.vector.scalar_tensor_tensor(result[:], excess[h][:], 0.0, excess[h][:], ALU.max, ALU.mult)
            nc.sync.dma_start(out[h * P : (h + 1) * P, :], result[:])
